import numpy as np
import ml_dtypes


def mxq(x, axis, fmt="e4m3"):
    dtype, down = {"e4m3": (ml_dtypes.float8_e4m3fn, 7), "e5m2": (ml_dtypes.float8_e5m2, 14)}[fmt]
    v = np.moveaxis(np.asarray(x, np.float32).astype(ml_dtypes.bfloat16).astype(np.float64), axis, -1)
    blocks = v.reshape(v.shape[:-1] + (-1, 32))
    amax = np.abs(blocks).max(-1, keepdims=True)
    byte = np.maximum(np.where(amax > 0, np.frexp(amax)[1] - 1 + 127, 0) - down, 1)
    scale = np.exp2(byte - 127.0)
    codes = (blocks / scale).astype(np.float32).astype(dtype).astype(np.float64)
    return np.moveaxis((codes * scale).reshape(v.shape), -1, axis)


WIDE = False


def mx_kscale(k):
    if not WIDE:
        return np.ones(k)
    levels = np.array([10, -10, 5, -5, 0])
    if k % 512:
        return np.exp2(np.random.permutation(np.resize(levels, k // 32))).repeat(32)
    a = np.empty((k // 512, 16))
    for p in range(k // 512):
        a[p, :8] = np.random.permutation(np.resize(levels, 8))
        for g in range(8):
            far = levels[np.abs(levels - a[p, g]) >= 10]
            a[p, g + 8] = far[np.random.randint(len(far))]
    return np.exp2(a.ravel()).repeat(32)


def f64(x):
    return np.asarray(x).astype(np.float64)


def striped(idx):
    return np.tile(idx.reshape(-1, 16).T, (8, 1)).astype(np.uint16)


def unstriped(offs):
    return offs[:16].T.reshape(-1).astype(np.int64)


def d_relu(v):
    return (v > 0).astype(np.float64)


K, T, E, C, H, N = 384, 512, 4, 256, 1024, 1024


def by_expert(wq, xq):
    return np.concatenate([wq[e].T @ xq[:, e * C:(e + 1) * C] for e in range(E)], axis=1)


def setup_inputs():
    n = np.random.standard_normal
    s = mx_kscale(N)[:, None]
    u = mx_kscale(H)
    first = np.random.permutation(np.repeat(np.arange(E), T // E))
    second = (first + 1 + np.random.permutation(np.repeat(np.arange(E - 1), -(-T // (E - 1)))[:T])) % E
    while np.bincount(second, minlength=E).max() != T // E:
        load = np.bincount(second, minlength=E); hi, lo = int(load.argmax()), int(load.argmin())
        t = np.flatnonzero((second == hi) & (first != lo))[0]; second[t] = lo
    slot_token = np.empty(E * C, np.int64); pos = np.empty((2, T), np.int64); fill = np.zeros(E, np.int64)
    place = np.stack([np.random.permutation(C) for _ in range(E)])
    for r, deal in enumerate((first, second)):
        for t in np.random.permutation(T):
            e = deal[t]; j = e * C + place[e, fill[e]]; fill[e] += 1; slot_token[j] = t; pos[r, t] = j
    g = np.random.uniform(0.2, 0.8, T)
    w_slot = np.empty(E * C); w_slot[pos[0]] = g; w_slot[pos[1]] = 1.0 - g
    return {
        "dyT": (n((N, T)) * s).astype(np.float32),
        "a": n((H, E * C)).astype(np.float32),
        "w2": (n((E, N, H)) / np.sqrt(N) / s[None] * u[None, None, :]).astype(np.float32),
        "w1": (n((E, H, K)) / np.sqrt(H) / u[None, :, None]).astype(np.float32),
        "gate": np.tile(w_slot, (N, 1)).astype(np.float32),
        "offs": striped(slot_token),
        "pos1": striped(pos[0]),
        "pos2": striped(pos[1]),
    }


def reference(dyT, a, w2, w1, gate, offs, pos1, pos2):
    idx = unstriped(offs)
    gq = mxq(f64(gate) * f64(dyT)[:, idx], 0, "e4m3")
    dh = by_expert(mxq(f64(w2), 1, "e4m3"), gq)
    da = dh * d_relu(f64(a))
    dx = by_expert(mxq(f64(w1), 1, "e4m3"), mxq(da, 0, "e4m3"))
    return dx[:, unstriped(pos1)] + dx[:, unstriped(pos2)]

@@ -1,0 +1,198 @@
+import concourse.mybir as mybir
+from contextlib import ExitStack
+
+N, H, K = 1024, 1024, 384
+TOKENS, EXPERTS, CAP = 512, 4, 256
+SLOTS = EXPERTS * CAP
+
+FLOPS = 2 * SLOTS * (N * H + H * K)
+BYTES = 4 * (N * TOKENS + H * SLOTS + EXPERTS * H * (N + K) + SLOTS + K * TOKENS) + 2 * 128 * (64 + 32 + 32)
+
+F32 = mybir.dt.float32
+BF16 = mybir.dt.bfloat16
+U32 = mybir.dt.uint32
+U16 = mybir.dt.uint16
+U8 = mybir.dt.uint8
+FP8X4 = mybir.dt.float8_e4m3fn_x4
+ALU = mybir.AluOpType
+
+P = 128
+S_SHARE = 96
+
+
+def tile_moe_bdx_mlp_relu_kernel(tc, dyT, a, w2, w1, gate, offs, pos1, pos2, out):
+    nc = tc.nc
+    with ExitStack() as ctx:
+        held = ctx.enter_context(tc.tile_pool(name="held", bufs=1))
+        raws = ctx.enter_context(tc.tile_pool(name="raws", bufs=4))
+        work = ctx.enter_context(tc.tile_pool(name="work", bufs=2))
+        quant = ctx.enter_context(tc.tile_pool(name="quant", bufs=4))
+        wide = ctx.enter_context(tc.tile_pool(name="wide", bufs=3))
+        psum_h = ctx.enter_context(tc.psum_pool(name="psum_h", bufs=6))
+        psum_x = ctx.enter_context(tc.psum_pool(name="psum_x", bufs=2))
+
+        offs_sb = held.tile([P, SLOTS // 16], U16, name="offs_sb")
+        pos1_sb = held.tile([P, TOKENS // 16], U16, name="pos1_sb")
+        pos2_sb = held.tile([P, TOKENS // 16], U16, name="pos2_sb")
+        gate_sb = held.tile([P, SLOTS], F32, name="gate_sb")
+        nc.sync.dma_start(offs_sb[:], offs)
+        nc.sync.dma_start(gate_sb[:], gate[0:P, :])
+        dy = {}
+        for c in range(2):
+            rows = dyT[c * 512 : (c + 1) * 512, :].rearrange("(p j) t -> p j t", j=4)
+            for j in range(4):
+                dy[c, j] = held.tile([P, TOKENS], F32, name=f"dy_{c}_{j}")
+                nc.sync.dma_start(dy[c, j][:], rows[:, j, :])
+
+        w2_raw = {}
+
+        def load_w2(e):
+            for c in range(2):
+                w2_raw[e, c] = raws.tile([P, 4, H], F32, name="raw", tag="raw")
+                nc.sync.dma_start(w2_raw[e, c][:], w2[e, c * 512 : (c + 1) * 512, :].rearrange("(p j) i -> p j i", j=4))
+
+        w1_raw = {}
+
+        def load_w1(e):
+            w1_raw[e] = raws.tile([P, 2, 4, K], F32, name="raw", tag="raw")
+            for c in range(2):
+                nc.sync.dma_start(w1_raw[e][:, c, :, :], w1[e, c * 512 : (c + 1) * 512, :].rearrange("(p j) k -> p j k", j=4))
+
+        g_codes = {}
+        g_scales = {}
+
+        def gather(e):
+            g_bf = work.tile([P, 2, CAP, 4], BF16, name="g_bf", align_bytes=64)
+            for c in range(2):
+                g32 = work.tile([P, 4, CAP], F32, name="g32")
+                for j in range(4):
+                    nc.vector.tensor_tensor(
+                        g32[:, j, :],
+                        dy[c, j][:].indirect(offs_sb[:, e * 16 : (e + 1) * 16]),
+                        gate_sb[:, e * CAP : (e + 1) * CAP],
+                        ALU.mult,
+                    )
+                nc.scalar.copy(
+                    g_bf[:, c, :, :].rearrange("p (s i) j -> p s j i", i=4),
+                    g32[:].rearrange("p j (s i) -> p s j i", i=4),
+                )
+            g_codes[e] = quant.tile([P, 2 * CAP], U32, name="g_codes", align_bytes=64)
+            g_scales[e] = quant.tile([P, 2 * CAP], U8, name="g_scales", align_bytes=64)
+            nc.vector.quantize_mx(g_codes[e][:].bitcast(FP8X4), g_scales[e][:], g_bf[:].rearrange("p c s j -> p (c s j)"))
+
+        w2_codes = {}
+        w2_scales = {}
+
+        def quant_w2(e, c):
+            w_bf = wide.tile([P, 4 * H], BF16, name="w_bf", align_bytes=64)
+            codes = quant.tile([P, H], U32, name="w_codes", align_bytes=64)
+            scales = quant.tile([P, H], U8, name="w_scales", align_bytes=64)
+            for ic in range(2):
+                dst = w_bf[:, ic * 2048 : (ic + 1) * 2048].rearrange("p (t m j) -> p m j t", t=4, j=4)
+                src = w2_raw[e, c][:, :, ic * 512 : (ic + 1) * 512].rearrange("p j (m t) -> p m j t", t=4)
+                nc.scalar.copy(dst[:, 0:S_SHARE], src[:, 0:S_SHARE])
+                nc.vector.tensor_copy(dst[:, S_SHARE:128], src[:, S_SHARE:128])
+                nc.vector.quantize_mx(
+                    codes[:, ic * 512 : (ic + 1) * 512].bitcast(FP8X4),
+                    scales[:, ic * 512 : (ic + 1) * 512],
+                    w_bf[:, ic * 2048 : (ic + 1) * 2048],
+                )
+            w2_codes[e, c] = codes
+            w2_scales[e, c] = scales
+
+        da_codes = {}
+        da_scales = {}
+
+        def hidden(e):
+            da_bf = work.tile([P, 2, CAP, 4], BF16, name="da_bf", align_bytes=64)
+            for ic in range(2):
+                for h in range(2):
+                    dh = psum_h.tile([P, 4, 128], F32, name="dh")
+                    for t in range(4):
+                        for c in range(2):
+                            cols = slice(ic * 512 + t * 128, ic * 512 + (t + 1) * 128)
+                            slots = slice(c * CAP + h * 128, c * CAP + (h + 1) * 128)
+                            nc.tensor.matmul_mx(
+                                dh[:, t, :],
+                                lhsT=w2_codes[e, c][:, cols].bitcast(FP8X4),
+                                lhsT_scale=w2_scales[e, c][:, cols],
+                                rhs=g_codes[e][:, slots].bitcast(FP8X4),
+                                rhs_scale=g_scales[e][:, slots],
+                                start=(c == 0),
+                                stop=(c == 1),
+                            )
+                    first = e * CAP + h * 128
+                    nc.vector.scalar_tensor_tensor(
+                        da_bf[:, ic, h * 128 : (h + 1) * 128, :],
+                        a_sb[ic][:, :, first : first + 128].rearrange("p t s -> p s t"),
+                        0.0,
+                        dh[:].rearrange("p t s -> p s t"),
+                        ALU.is_gt,
+                        ALU.mult,
+                    )
+            da_codes[e] = quant.tile([P, 2 * CAP], U32, name="da_codes", align_bytes=64)
+            da_scales[e] = quant.tile([P, 2 * CAP], U8, name="da_scales", align_bytes=64)
+            nc.vector.quantize_mx(da_codes[e][:].bitcast(FP8X4), da_scales[e][:], da_bf[:].rearrange("p c s j -> p (c s j)"))
+
+        dx = [held.tile([P, SLOTS], F32, name=f"dx_{kt}") for kt in range(3)]
+
+        def project(e):
+            w_bf = wide.tile([P, 3, 2, 128, 4], BF16, name="w_bf", align_bytes=64)
+            codes = quant.tile([P, 3, 2, 128], U32, name="w_codes", align_bytes=64)
+            scales = quant.tile([P, 3, 2, 128], U8, name="w_scales", align_bytes=64)
+            for ic in range(2):
+                for kt in range(3):
+                    dst = w_bf[:, kt, ic, :, :].rearrange("p (k i) j -> p k j i", i=4)
+                    src = w1_raw[e][:, ic, :, kt * 128 : (kt + 1) * 128].rearrange("p j (k i) -> p k j i", i=4)
+                    if kt == 2:
+                        nc.vector.tensor_copy(dst, src)
+                    else:
+                        nc.scalar.copy(dst, src)
+            flat = w_bf[:].rearrange("p a b k j -> p (a b k j)")
+            flat_codes = codes[:].rearrange("p a b k -> p (a b k)")
+            flat_scales = scales[:].rearrange("p a b k -> p (a b k)")
+            for lo, hi in ((0, 512), (512, 768)):
+                nc.vector.quantize_mx(flat_codes[:, lo:hi].bitcast(FP8X4), flat_scales[:, lo:hi], flat[:, 4 * lo : 4 * hi])
+            for kt in range(3):
+                acc = psum_x.tile([P, CAP], F32, name="acc")
+                for ic in range(2):
+                    nc.tensor.matmul_mx(
+                        acc[:],
+                        lhsT=codes[:, kt, ic, :].bitcast(FP8X4),
+                        lhsT_scale=scales[:, kt, ic, :],
+                        rhs=da_codes[e][:, ic * CAP : (ic + 1) * CAP].bitcast(FP8X4),
+                        rhs_scale=da_scales[e][:, ic * CAP : (ic + 1) * CAP],
+                        start=(ic == 0),
+                        stop=(ic == 1),
+                    )
+                nc.scalar.copy(dx[kt][:, e * CAP : (e + 1) * CAP], acc[:])
+
+        load_w2(0)
+        a_sb = []
+        for ic in range(2):
+            chunk = held.tile([P, 4, SLOTS], F32, name=f"a_{ic}")
+            nc.sync.dma_start(chunk[:], a[ic * 512 : (ic + 1) * 512, :].rearrange("(p t) s -> p t s", t=4))
+            a_sb.append(chunk)
+        nc.sync.dma_start(pos1_sb[:], pos1)
+        nc.sync.dma_start(pos2_sb[:], pos2)
+
+        gather(0)
+        for e in range(EXPERTS):
+            if e > 0:
+                load_w2(e)
+            quant_w2(e, 0)
+            if e + 1 < EXPERTS:
+                gather(e + 1)
+            quant_w2(e, 1)
+            hidden(e)
+        for e in range(EXPERTS):
+            load_w1(e)
+            project(e)
+        for kt in range(3):
+            first = work.tile([P, TOKENS], F32, name="first")
+            second = work.tile([P, TOKENS], F32, name="second")
+            nc.vector.tensor_copy(first[:], dx[kt][:].indirect(pos1_sb[:]))
+            nc.vector.tensor_copy(second[:], dx[kt][:].indirect(pos2_sb[:]))
+            total = work.tile([P, TOKENS], F32, name="total")
+            nc.vector.tensor_add(total[:], first[:], second[:])
+            nc.sync.dma_start(out[kt * 128 : (kt + 1) * 128, :], total[:])

@@ -17,17 +17,17 @@ FP8X4 = mybir.dt.float8_e4m3fn_x4
 ALU = mybir.AluOpType
 
 P = 128
-S_SHARE = 96
 
 
 def tile_moe_bdx_mlp_relu_kernel(tc, dyT, a, w2, w1, gate, offs, pos1, pos2, out):
     nc = tc.nc
     with ExitStack() as ctx:
         held = ctx.enter_context(tc.tile_pool(name="held", bufs=1))
-        raws = ctx.enter_context(tc.tile_pool(name="raws", bufs=4))
+        raws = ctx.enter_context(tc.tile_pool(name="raws", bufs=5))
         work = ctx.enter_context(tc.tile_pool(name="work", bufs=2))
         quant = ctx.enter_context(tc.tile_pool(name="quant", bufs=4))
         wide = ctx.enter_context(tc.tile_pool(name="wide", bufs=3))
+        gathered = ctx.enter_context(tc.tile_pool(name="gathered", bufs=3))
         psum_h = ctx.enter_context(tc.psum_pool(name="psum_h", bufs=6))
         psum_x = ctx.enter_context(tc.psum_pool(name="psum_x", bufs=2))
 
@@ -38,7 +38,8 @@ def tile_moe_bdx_mlp_relu_kernel(tc, dyT, a, w2, w1, gate, offs, pos1, pos2, out
         nc.sync.dma_start(offs_sb[:], offs)
         nc.sync.dma_start(gate_sb[:], gate[0:P, :])
         dy = {}
-        for c in range(2):
+
+        def load_dy(c):
             rows = dyT[c * 512 : (c + 1) * 512, :].rearrange("(p j) t -> p j t", j=4)
             for j in range(4):
                 dy[c, j] = held.tile([P, TOKENS], F32, name=f"dy_{c}_{j}")
@@ -46,10 +47,19 @@ def tile_moe_bdx_mlp_relu_kernel(tc, dyT, a, w2, w1, gate, offs, pos1, pos2, out
 
         w2_raw = {}
 
-        def load_w2(e):
-            for c in range(2):
-                w2_raw[e, c] = raws.tile([P, 4, H], F32, name="raw", tag="raw")
-                nc.sync.dma_start(w2_raw[e, c][:], w2[e, c * 512 : (c + 1) * 512, :].rearrange("(p j) i -> p j i", j=4))
+        def load_w2(e, c):
+            rows = w2[e, c * 512 : (c + 1) * 512, :].rearrange("(p j) i -> p j i", j=4)
+            if (e, c) == (0, 0):
+                halves = []
+                for ic in range(2):
+                    half = raws.tile([P, 4, 512], F32, name="raw", tag="raw")
+                    nc.sync.dma_start(half[:], rows[:, :, ic * 512 : (ic + 1) * 512])
+                    halves.append(half[:])
+            else:
+                whole = raws.tile([P, 4, H], F32, name="raw", tag="raw")
+                nc.sync.dma_start(whole[:], rows)
+                halves = [whole[:, :, 0:512], whole[:, :, 512:1024]]
+            w2_raw[e, c] = halves
 
         w1_raw = {}
 
@@ -64,7 +74,7 @@ def tile_moe_bdx_mlp_relu_kernel(tc, dyT, a, w2, w1, gate, offs, pos1, pos2, out
         def gather(e):
             g_bf = work.tile([P, 2, CAP, 4], BF16, name="g_bf", align_bytes=64)
             for c in range(2):
-                g32 = work.tile([P, 4, CAP], F32, name="g32")
+                g32 = gathered.tile([P, 4, CAP], F32, name="g32")
                 for j in range(4):
                     nc.vector.tensor_tensor(
                         g32[:, j, :],
@@ -72,7 +82,7 @@ def tile_moe_bdx_mlp_relu_kernel(tc, dyT, a, w2, w1, gate, offs, pos1, pos2, out
                         gate_sb[:, e * CAP : (e + 1) * CAP],
                         ALU.mult,
                     )
-                nc.scalar.copy(
+                nc.vector.tensor_copy(
                     g_bf[:, c, :, :].rearrange("p (s i) j -> p s j i", i=4),
                     g32[:].rearrange("p j (s i) -> p s j i", i=4),
                 )
@@ -89,14 +99,19 @@ def tile_moe_bdx_mlp_relu_kernel(tc, dyT, a, w2, w1, gate, offs, pos1, pos2, out
             scales = quant.tile([P, H], U8, name="w_scales", align_bytes=64)
             for ic in range(2):
                 dst = w_bf[:, ic * 2048 : (ic + 1) * 2048].rearrange("p (t m j) -> p m j t", t=4, j=4)
-                src = w2_raw[e, c][:, :, ic * 512 : (ic + 1) * 512].rearrange("p j (m t) -> p m j t", t=4)
-                nc.scalar.copy(dst[:, 0:S_SHARE], src[:, 0:S_SHARE])
-                nc.vector.tensor_copy(dst[:, S_SHARE:128], src[:, S_SHARE:128])
-                nc.vector.quantize_mx(
-                    codes[:, ic * 512 : (ic + 1) * 512].bitcast(FP8X4),
-                    scales[:, ic * 512 : (ic + 1) * 512],
-                    w_bf[:, ic * 2048 : (ic + 1) * 2048],
-                )
+                src = w2_raw[e, c][ic].rearrange("p j (m t) -> p m j t", t=4)
+                v = 32 if (e, c) == (3, 1) else 0
+                nc.scalar.copy(dst[:, v:], src[:, v:])
+                if v:
+                    nc.vector.tensor_copy(dst[:, 0:v], src[:, 0:v])
+                if e == 3:
+                    nc.vector.quantize_mx(
+                        codes[:, ic * 512 : (ic + 1) * 512].bitcast(FP8X4),
+                        scales[:, ic * 512 : (ic + 1) * 512],
+                        w_bf[:, ic * 2048 : (ic + 1) * 2048],
+                    )
+            if e < 3:
+                nc.vector.quantize_mx(codes[:].bitcast(FP8X4), scales[:], w_bf[:])
             w2_codes[e, c] = codes
             w2_scales[e, c] = scales
 
@@ -121,10 +136,10 @@ def tile_moe_bdx_mlp_relu_kernel(tc, dyT, a, w2, w1, gate, offs, pos1, pos2, out
                                 start=(c == 0),
                                 stop=(c == 1),
                             )
-                    first = e * CAP + h * 128
+                    first = e % 2 * CAP + h * 128
                     nc.vector.scalar_tensor_tensor(
                         da_bf[:, ic, h * 128 : (h + 1) * 128, :],
-                        a_sb[ic][:, :, first : first + 128].rearrange("p t s -> p s t"),
+                        a_sb[ic, e // 2][:, :, first : first + 128].rearrange("p t s -> p s t"),
                         0.0,
                         dh[:].rearrange("p t s -> p s t"),
                         ALU.is_gt,
@@ -136,63 +151,103 @@ def tile_moe_bdx_mlp_relu_kernel(tc, dyT, a, w2, w1, gate, offs, pos1, pos2, out
 
         dx = [held.tile([P, SLOTS], F32, name=f"dx_{kt}") for kt in range(3)]
 
-        def project(e):
-            w_bf = wide.tile([P, 3, 2, 128, 4], BF16, name="w_bf", align_bytes=64)
-            codes = quant.tile([P, 3, 2, 128], U32, name="w_codes", align_bytes=64)
-            scales = quant.tile([P, 3, 2, 128], U8, name="w_scales", align_bytes=64)
-            for ic in range(2):
-                for kt in range(3):
-                    dst = w_bf[:, kt, ic, :, :].rearrange("p (k i) j -> p k j i", i=4)
-                    src = w1_raw[e][:, ic, :, kt * 128 : (kt + 1) * 128].rearrange("p j (k i) -> p k j i", i=4)
-                    if kt == 2:
-                        nc.vector.tensor_copy(dst, src)
-                    else:
-                        nc.scalar.copy(dst, src)
-            flat = w_bf[:].rearrange("p a b k j -> p (a b k j)")
+        w1_bf, w1_codes, w1_scales = {}, {}, {}
+
+        def cast_w1(e):
+            by_kt = e == EXPERTS - 1
+            shape = [P, 3, 2, 128] if by_kt else [P, 2, 3, 128]
+            w_bf = wide.tile(shape + [4], BF16, name="w_bf", align_bytes=64)
+            codes = quant.tile(shape, U32, name="w_codes", align_bytes=64)
+            scales = quant.tile(shape, U8, name="w_scales", align_bytes=64)
+            w1_bf[e] = w_bf[:].rearrange("p a b k j -> p (a b k j)")
             flat_codes = codes[:].rearrange("p a b k -> p (a b k)")
             flat_scales = scales[:].rearrange("p a b k -> p (a b k)")
-            for lo, hi in ((0, 512), (512, 768)):
-                nc.vector.quantize_mx(flat_codes[:, lo:hi].bitcast(FP8X4), flat_scales[:, lo:hi], flat[:, 4 * lo : 4 * hi])
-            for kt in range(3):
-                acc = psum_x.tile([P, CAP], F32, name="acc")
+            for lo, hi in ((0, 256), (256, 512), (512, 768)) if by_kt else ((0, 512), (512, 768)):
                 for ic in range(2):
-                    nc.tensor.matmul_mx(
-                        acc[:],
-                        lhsT=codes[:, kt, ic, :].bitcast(FP8X4),
-                        lhsT_scale=scales[:, kt, ic, :],
-                        rhs=da_codes[e][:, ic * CAP : (ic + 1) * CAP].bitcast(FP8X4),
-                        rhs_scale=da_scales[e][:, ic * CAP : (ic + 1) * CAP],
-                        start=(ic == 0),
-                        stop=(ic == 1),
-                    )
-                nc.scalar.copy(dx[kt][:, e * CAP : (e + 1) * CAP], acc[:])
+                    copy = nc.vector.tensor_copy if ic else nc.scalar.copy
+                    if by_kt:
+                        kt = lo // 256
+                        copy(
+                            w_bf[:, kt, ic, :, :].rearrange("p (k i) j -> p k j i", i=4),
+                            w1_raw[e][:, ic, :, kt * 128 : (kt + 1) * 128].rearrange("p j (k i) -> p k j i", i=4),
+                        )
+                    elif lo == 0:
+                        copy(
+                            w_bf[:, ic, :, :, :].rearrange("p a (k i) j -> p (a k) j i", i=4),
+                            w1_raw[e][:, ic, :, :].rearrange("p j (k i) -> p k j i", i=4),
+                        )
+                nc.vector.quantize_mx(flat_codes[:, lo:hi].bitcast(FP8X4), flat_scales[:, lo:hi], w1_bf[e][:, 4 * lo : 4 * hi])
+            for kt in range(3):
+                for ic in range(2):
+                    at = (kt, ic) if by_kt else (ic, kt)
+                    w1_codes[e, kt, ic] = codes[:, at[0], at[1], :]
+                    w1_scales[e, kt, ic] = scales[:, at[0], at[1], :]
 
-        load_w2(0)
-        a_sb = []
-        for ic in range(2):
-            chunk = held.tile([P, 4, SLOTS], F32, name=f"a_{ic}")
-            nc.sync.dma_start(chunk[:], a[ic * 512 : (ic + 1) * 512, :].rearrange("(p t) s -> p t s", t=4))
-            a_sb.append(chunk)
-        nc.sync.dma_start(pos1_sb[:], pos1)
-        nc.sync.dma_start(pos2_sb[:], pos2)
+        def project(e, kt):
+            acc = psum_x.tile([P, CAP], F32, name="acc")
+            for ic in range(2):
+                nc.tensor.matmul_mx(
+                    acc[:],
+                    lhsT=w1_codes[e, kt, ic].bitcast(FP8X4),
+                    lhsT_scale=w1_scales[e, kt, ic],
+                    rhs=da_codes[e][:, ic * CAP : (ic + 1) * CAP].bitcast(FP8X4),
+                    rhs_scale=da_scales[e][:, ic * CAP : (ic + 1) * CAP],
+                    start=(ic == 0),
+                    stop=(ic == 1),
+                )
+            nc.scalar.copy(dx[kt][:, e * CAP : (e + 1) * CAP], acc[:])
 
-        gather(0)
-        for e in range(EXPERTS):
-            if e > 0:
-                load_w2(e)
-            quant_w2(e, 0)
-            if e + 1 < EXPERTS:
-                gather(e + 1)
-            quant_w2(e, 1)
-            hidden(e)
-        for e in range(EXPERTS):
-            load_w1(e)
-            project(e)
-        for kt in range(3):
+        def combine(kt):
             first = work.tile([P, TOKENS], F32, name="first")
             second = work.tile([P, TOKENS], F32, name="second")
             nc.vector.tensor_copy(first[:], dx[kt][:].indirect(pos1_sb[:]))
             nc.vector.tensor_copy(second[:], dx[kt][:].indirect(pos2_sb[:]))
             total = work.tile([P, TOKENS], F32, name="total")
-            nc.vector.tensor_add(total[:], first[:], second[:])
+            adder = nc.vector if kt == 2 else nc.gpsimd
+            adder.tensor_tensor(total[:], first[:], second[:], ALU.add)
             nc.sync.dma_start(out[kt * 128 : (kt + 1) * 128, :], total[:])
+
+        a_sb = {}
+
+        def load_a(half):
+            cols = slice(half * 2 * CAP, (half + 1) * 2 * CAP)
+            for ic in range(2):
+                a_sb[ic, half] = work.tile([P, 4, 2 * CAP], F32, name="a_half")
+                nc.sync.dma_start(a_sb[ic, half][:], a[ic * 512 : (ic + 1) * 512, cols].rearrange("(p t) s -> p t s", t=4))
+
+        load_dy(0)
+        load_w2(0, 0)
+        load_dy(1)
+        load_w2(0, 1)
+        load_w2(1, 0)
+        load_a(0)
+        load_w2(1, 1)
+        nc.sync.dma_start(pos1_sb[:], pos1)
+        nc.sync.dma_start(pos2_sb[:], pos2)
+
+        def load_after(e, c):
+            if (e, c) == (0, 0):
+                load_w2(2, 0)
+                load_w2(2, 1)
+            elif 2 * e + c + 5 < 8:
+                load_w2((2 * e + c + 5) // 2, 1 - c)
+            elif 2 * e + c - 3 < EXPERTS:
+                load_w1(2 * e + c - 3)
+
+        gather(0)
+        for e in range(EXPERTS):
+            quant_w2(e, 0)
+            load_after(e, 0)
+            if e + 1 < EXPERTS:
+                gather(e + 1)
+            quant_w2(e, 1)
+            load_after(e, 1)
+            hidden(e)
+            if e == 1:
+                load_a(1)
+        for e in range(EXPERTS):
+            cast_w1(e)
+            for kt in range(3):
+                project(e, kt)
+                if e == EXPERTS - 1:
+                    combine(kt)

import concourse.mybir as mybir
from contextlib import ExitStack

N, H, K = 1024, 1024, 384
TOKENS, EXPERTS, CAP = 512, 4, 256
SLOTS = EXPERTS * CAP

FLOPS = 2 * SLOTS * (N * H + H * K)
BYTES = 4 * (N * TOKENS + H * SLOTS + EXPERTS * H * (N + K) + SLOTS + K * TOKENS) + 2 * 128 * (64 + 32 + 32)

F32 = mybir.dt.float32
BF16 = mybir.dt.bfloat16
U32 = mybir.dt.uint32
U16 = mybir.dt.uint16
U8 = mybir.dt.uint8
FP8X4 = mybir.dt.float8_e4m3fn_x4
ALU = mybir.AluOpType

P = 128


def tile_moe_bdx_mlp_relu_kernel(tc, dyT, a, w2, w1, gate, offs, pos1, pos2, out):
    nc = tc.nc
    with ExitStack() as ctx:
        held = ctx.enter_context(tc.tile_pool(name="held", bufs=1))
        raws = ctx.enter_context(tc.tile_pool(name="raws", bufs=5))
        work = ctx.enter_context(tc.tile_pool(name="work", bufs=2))
        quant = ctx.enter_context(tc.tile_pool(name="quant", bufs=4))
        wide = ctx.enter_context(tc.tile_pool(name="wide", bufs=3))
        gathered = ctx.enter_context(tc.tile_pool(name="gathered", bufs=3))
        psum_h = ctx.enter_context(tc.psum_pool(name="psum_h", bufs=6))
        psum_x = ctx.enter_context(tc.psum_pool(name="psum_x", bufs=2))

        offs_sb = held.tile([P, SLOTS // 16], U16, name="offs_sb")
        pos1_sb = held.tile([P, TOKENS // 16], U16, name="pos1_sb")
        pos2_sb = held.tile([P, TOKENS // 16], U16, name="pos2_sb")
        gate_sb = held.tile([P, SLOTS], F32, name="gate_sb")
        nc.sync.dma_start(offs_sb[:], offs)
        nc.sync.dma_start(gate_sb[:], gate[0:P, :])
        dy = {}

        def load_dy(c):
            rows = dyT[c * 512 : (c + 1) * 512, :].rearrange("(p j) t -> p j t", j=4)
            for j in range(4):
                dy[c, j] = held.tile([P, TOKENS], F32, name=f"dy_{c}_{j}")
                nc.sync.dma_start(dy[c, j][:], rows[:, j, :])

        w2_raw = {}

        def load_w2(e, c):
            rows = w2[e, c * 512 : (c + 1) * 512, :].rearrange("(p j) i -> p j i", j=4)
            if (e, c) == (0, 0):
                halves = []
                for ic in range(2):
                    half = raws.tile([P, 4, 512], F32, name="raw", tag="raw")
                    nc.sync.dma_start(half[:], rows[:, :, ic * 512 : (ic + 1) * 512])
                    halves.append(half[:])
            else:
                whole = raws.tile([P, 4, H], F32, name="raw", tag="raw")
                nc.sync.dma_start(whole[:], rows)
                halves = [whole[:, :, 0:512], whole[:, :, 512:1024]]
            w2_raw[e, c] = halves

        w1_raw = {}

        def load_w1(e):
            w1_raw[e] = raws.tile([P, 2, 4, K], F32, name="raw", tag="raw")
            for c in range(2):
                nc.sync.dma_start(w1_raw[e][:, c, :, :], w1[e, c * 512 : (c + 1) * 512, :].rearrange("(p j) k -> p j k", j=4))

        g_codes = {}
        g_scales = {}

        def gather(e):
            g_bf = work.tile([P, 2, CAP, 4], BF16, name="g_bf", align_bytes=64)
            for c in range(2):
                g32 = gathered.tile([P, 4, CAP], F32, name="g32")
                for j in range(4):
                    nc.vector.tensor_tensor(
                        g32[:, j, :],
                        dy[c, j][:].indirect(offs_sb[:, e * 16 : (e + 1) * 16]),
                        gate_sb[:, e * CAP : (e + 1) * CAP],
                        ALU.mult,
                    )
                nc.vector.tensor_copy(
                    g_bf[:, c, :, :].rearrange("p (s i) j -> p s j i", i=4),
                    g32[:].rearrange("p j (s i) -> p s j i", i=4),
                )
            g_codes[e] = quant.tile([P, 2 * CAP], U32, name="g_codes", align_bytes=64)
            g_scales[e] = quant.tile([P, 2 * CAP], U8, name="g_scales", align_bytes=64)
            nc.vector.quantize_mx(g_codes[e][:].bitcast(FP8X4), g_scales[e][:], g_bf[:].rearrange("p c s j -> p (c s j)"))

        w2_codes = {}
        w2_scales = {}

        def quant_w2(e, c):
            w_bf = wide.tile([P, 4 * H], BF16, name="w_bf", align_bytes=64)
            codes = quant.tile([P, H], U32, name="w_codes", align_bytes=64)
            scales = quant.tile([P, H], U8, name="w_scales", align_bytes=64)
            for ic in range(2):
                dst = w_bf[:, ic * 2048 : (ic + 1) * 2048].rearrange("p (t m j) -> p m j t", t=4, j=4)
                src = w2_raw[e, c][ic].rearrange("p j (m t) -> p m j t", t=4)
                v = 32 if (e, c) == (3, 1) else 0
                nc.scalar.copy(dst[:, v:], src[:, v:])
                if v:
                    nc.vector.tensor_copy(dst[:, 0:v], src[:, 0:v])
                if e == 3:
                    nc.vector.quantize_mx(
                        codes[:, ic * 512 : (ic + 1) * 512].bitcast(FP8X4),
                        scales[:, ic * 512 : (ic + 1) * 512],
                        w_bf[:, ic * 2048 : (ic + 1) * 2048],
                    )
            if e < 3:
                nc.vector.quantize_mx(codes[:].bitcast(FP8X4), scales[:], w_bf[:])
            w2_codes[e, c] = codes
            w2_scales[e, c] = scales

        da_codes = {}
        da_scales = {}

        def hidden(e):
            da_bf = work.tile([P, 2, CAP, 4], BF16, name="da_bf", align_bytes=64)
            for ic in range(2):
                for h in range(2):
                    dh = psum_h.tile([P, 4, 128], F32, name="dh")
                    for t in range(4):
                        for c in range(2):
                            cols = slice(ic * 512 + t * 128, ic * 512 + (t + 1) * 128)
                            slots = slice(c * CAP + h * 128, c * CAP + (h + 1) * 128)
                            nc.tensor.matmul_mx(
                                dh[:, t, :],
                                lhsT=w2_codes[e, c][:, cols].bitcast(FP8X4),
                                lhsT_scale=w2_scales[e, c][:, cols],
                                rhs=g_codes[e][:, slots].bitcast(FP8X4),
                                rhs_scale=g_scales[e][:, slots],
                                start=(c == 0),
                                stop=(c == 1),
                            )
                    first = e % 2 * CAP + h * 128
                    nc.vector.scalar_tensor_tensor(
                        da_bf[:, ic, h * 128 : (h + 1) * 128, :],
                        a_sb[ic, e // 2][:, :, first : first + 128].rearrange("p t s -> p s t"),
                        0.0,
                        dh[:].rearrange("p t s -> p s t"),
                        ALU.is_gt,
                        ALU.mult,
                    )
            da_codes[e] = quant.tile([P, 2 * CAP], U32, name="da_codes", align_bytes=64)
            da_scales[e] = quant.tile([P, 2 * CAP], U8, name="da_scales", align_bytes=64)
            nc.vector.quantize_mx(da_codes[e][:].bitcast(FP8X4), da_scales[e][:], da_bf[:].rearrange("p c s j -> p (c s j)"))

        dx = [held.tile([P, SLOTS], F32, name=f"dx_{kt}") for kt in range(3)]

        w1_bf, w1_codes, w1_scales = {}, {}, {}

        def cast_w1(e):
            by_kt = e == EXPERTS - 1
            shape = [P, 3, 2, 128] if by_kt else [P, 2, 3, 128]
            w_bf = wide.tile(shape + [4], BF16, name="w_bf", align_bytes=64)
            codes = quant.tile(shape, U32, name="w_codes", align_bytes=64)
            scales = quant.tile(shape, U8, name="w_scales", align_bytes=64)
            w1_bf[e] = w_bf[:].rearrange("p a b k j -> p (a b k j)")
            flat_codes = codes[:].rearrange("p a b k -> p (a b k)")
            flat_scales = scales[:].rearrange("p a b k -> p (a b k)")
            for lo, hi in ((0, 256), (256, 512), (512, 768)) if by_kt else ((0, 512), (512, 768)):
                for ic in range(2):
                    copy = nc.vector.tensor_copy if ic else nc.scalar.copy
                    if by_kt:
                        kt = lo // 256
                        copy(
                            w_bf[:, kt, ic, :, :].rearrange("p (k i) j -> p k j i", i=4),
                            w1_raw[e][:, ic, :, kt * 128 : (kt + 1) * 128].rearrange("p j (k i) -> p k j i", i=4),
                        )
                    elif lo == 0:
                        copy(
                            w_bf[:, ic, :, :, :].rearrange("p a (k i) j -> p (a k) j i", i=4),
                            w1_raw[e][:, ic, :, :].rearrange("p j (k i) -> p k j i", i=4),
                        )
                nc.vector.quantize_mx(flat_codes[:, lo:hi].bitcast(FP8X4), flat_scales[:, lo:hi], w1_bf[e][:, 4 * lo : 4 * hi])
            for kt in range(3):
                for ic in range(2):
                    at = (kt, ic) if by_kt else (ic, kt)
                    w1_codes[e, kt, ic] = codes[:, at[0], at[1], :]
                    w1_scales[e, kt, ic] = scales[:, at[0], at[1], :]

        def project(e, kt):
            acc = psum_x.tile([P, CAP], F32, name="acc")
            for ic in range(2):
                nc.tensor.matmul_mx(
                    acc[:],
                    lhsT=w1_codes[e, kt, ic].bitcast(FP8X4),
                    lhsT_scale=w1_scales[e, kt, ic],
                    rhs=da_codes[e][:, ic * CAP : (ic + 1) * CAP].bitcast(FP8X4),
                    rhs_scale=da_scales[e][:, ic * CAP : (ic + 1) * CAP],
                    start=(ic == 0),
                    stop=(ic == 1),
                )
            nc.scalar.copy(dx[kt][:, e * CAP : (e + 1) * CAP], acc[:])

        def combine(kt):
            first = work.tile([P, TOKENS], F32, name="first")
            second = work.tile([P, TOKENS], F32, name="second")
            nc.vector.tensor_copy(first[:], dx[kt][:].indirect(pos1_sb[:]))
            nc.vector.tensor_copy(second[:], dx[kt][:].indirect(pos2_sb[:]))
            total = work.tile([P, TOKENS], F32, name="total")
            adder = nc.vector if kt == 2 else nc.gpsimd
            adder.tensor_tensor(total[:], first[:], second[:], ALU.add)
            nc.sync.dma_start(out[kt * 128 : (kt + 1) * 128, :], total[:])

        a_sb = {}

        def load_a(half):
            cols = slice(half * 2 * CAP, (half + 1) * 2 * CAP)
            for ic in range(2):
                a_sb[ic, half] = work.tile([P, 4, 2 * CAP], F32, name="a_half")
                nc.sync.dma_start(a_sb[ic, half][:], a[ic * 512 : (ic + 1) * 512, cols].rearrange("(p t) s -> p t s", t=4))

        load_dy(0)
        load_w2(0, 0)
        load_dy(1)
        load_w2(0, 1)
        load_w2(1, 0)
        load_a(0)
        load_w2(1, 1)
        nc.sync.dma_start(pos1_sb[:], pos1)
        nc.sync.dma_start(pos2_sb[:], pos2)

        def load_after(e, c):
            if (e, c) == (0, 0):
                load_w2(2, 0)
                load_w2(2, 1)
            elif 2 * e + c + 5 < 8:
                load_w2((2 * e + c + 5) // 2, 1 - c)
            elif 2 * e + c - 3 < EXPERTS:
                load_w1(2 * e + c - 3)

        gather(0)
        for e in range(EXPERTS):
            quant_w2(e, 0)
            load_after(e, 0)
            if e + 1 < EXPERTS:
                gather(e + 1)
            quant_w2(e, 1)
            load_after(e, 1)
            hidden(e)
            if e == 1:
                load_a(1)
        for e in range(EXPERTS):
            cast_w1(e)
            for kt in range(3):
                project(e, kt)
                if e == EXPERTS - 1:
                    combine(kt)
